import numpy as np
import ml_dtypes


def mxq(x, axis, fmt="e4m3"):
    dtype, down = {"e4m3": (ml_dtypes.float8_e4m3fn, 7), "e5m2": (ml_dtypes.float8_e5m2, 14)}[fmt]
    v = np.moveaxis(np.asarray(x, np.float32).astype(ml_dtypes.bfloat16).astype(np.float64), axis, -1)
    blocks = v.reshape(v.shape[:-1] + (-1, 32))
    amax = np.abs(blocks).max(-1, keepdims=True)
    byte = np.maximum(np.where(amax > 0, np.frexp(amax)[1] - 1 + 127, 0) - down, 1)
    scale = np.exp2(byte - 127.0)
    codes = (blocks / scale).astype(np.float32).astype(dtype).astype(np.float64)
    return np.moveaxis((codes * scale).reshape(v.shape), -1, axis)


WIDE = False


def mx_kscale(k):
    if not WIDE:
        return np.ones(k)
    levels = np.array([30, -30])
    if k % 512:
        return np.exp2(np.random.permutation(np.resize(levels, k // 32))).repeat(32)
    a = np.empty((k // 512, 16))
    for p in range(k // 512):
        a[p, :8] = np.random.permutation(np.resize(levels, 8))
        for g in range(8):
            far = levels[np.abs(levels - a[p, g]) >= 10]
            a[p, g + 8] = far[np.random.randint(len(far))]
    return np.exp2(a.ravel()).repeat(32)


BF16 = ml_dtypes.bfloat16


def bf(x):
    return np.asarray(x, np.float32).astype(BF16)


def f64(x):
    return np.asarray(x).astype(np.float64)


P, C, D, T = 1024, 512, 2, 1024


def setup_inputs():
    s, t = mx_kscale(C), mx_kscale(P)
    heavy = np.random.standard_normal((P, D, T)) * np.exp(np.random.standard_normal((P, D, T)) - 1.0)
    g = np.random.standard_normal((P, D, T))
    norm = np.sqrt(1.0 + np.square(g).sum(axis=1))
    return {"prolong": bf(np.random.standard_normal((P, C)) / np.sqrt(C) / s),
            "coarse": bf(np.random.standard_normal((C, D, T)) * s[:, None, None]),
            "average": bf(np.random.standard_normal((P, P)) / np.sqrt(P) / t),
            "step": bf(heavy * t[:, None, None]),
            "grad": bf(g / norm[:, None, :]),
            "dt": bf(np.random.standard_normal((P, T)) / norm)}


def reference(prolong, coarse, average, step, grad, dt):
    cq = mxq(f64(coarse).reshape(C, D * T), 0, "e4m3")
    sq = mxq(f64(step).reshape(P, D * T), 0, "e5m2")
    pq = mxq(f64(prolong), 1, "e4m3")
    aq = mxq(f64(average), 1, "e4m3")
    fbar = ((pq @ cq) + (aq @ sq)).reshape(P, D, T)
    g = f64(grad)
    r = (g * fbar).sum(axis=1) + f64(dt)
    flow = fbar - g * r[:, None, :]
    return flow, r

@@ -1,0 +1,246 @@
+from contextlib import ExitStack
+
+import concourse.mybir as mybir
+from concourse.masks import make_identity
+
+F32 = mybir.dt.float32
+BF16 = mybir.dt.bfloat16
+U32 = mybir.dt.uint32
+U8 = mybir.dt.uint8
+E4M3 = mybir.dt.float8_e4m3fn_x4
+E5M2 = mybir.dt.float8_e5m2_x4
+ADD = mybir.AluOpType.add
+SUB = mybir.AluOpType.subtract
+MUL = mybir.AluOpType.mult
+
+NODES, COARSE, COMPS, PAIRS = 1024, 512, 2, 1024
+FLOPS = 2 * NODES * COMPS * PAIRS * (COARSE + NODES)
+
+P = 128
+PACK = 4
+K_PASS = P * PACK
+N = 512
+PASSES = (COARSE + NODES) // K_PASS
+M_TILES = NODES // P
+HALVES = PAIRS // N
+TILES = M_TILES * HALVES
+V_COLS = 256
+PE_FROM = 8
+
+
+def tile_pyramid_horn_schunck_step_s2_kernel(tc, prolong, coarse, average, step, grad, dt, out_0, out_1):
+    nc = tc.nc
+    with ExitStack() as ctx:
+        keep = ctx.enter_context(tc.tile_pool(name="keep", bufs=1))
+        work = ctx.enter_context(tc.tile_pool(name="work", bufs=2))
+        psum = ctx.enter_context(tc.psum_pool(name="psum", bufs=1))
+        ctx.enter_context(tc.manual_schedule())
+
+        ident = keep.tile([P, P], F32, name="ident")
+        make_identity(nc, ident[:])
+        ident_bf = keep.tile([P, P], BF16, name="ident_bf")
+        nc.scalar.copy(out=ident_bf[:], in_=ident[:])
+
+        w_raw, g_sb, dt_sb, raw = {}, {}, {}, {}
+
+        def load_weights(m):
+            rows = slice(m * P, (m + 1) * P)
+            wp = keep.tile([P, COARSE], BF16, name="wp%d" % m)
+            wa = keep.tile([P, NODES], BF16, name="wa%d" % m)
+            nc.sync.dma_start(out=wp[:], in_=prolong[rows, :])
+            nc.sync.dma_start(out=wa[:], in_=average[rows, :])
+            w_raw[m] = (wp, wa)
+
+        def load_grad(m):
+            rows = slice(m * P, (m + 1) * P)
+            g_sb[m] = keep.tile([P, COMPS, PAIRS], BF16, name="g%d" % m)
+            nc.sync.dma_start(out=g_sb[m][:], in_=grad[rows])
+
+        def load_dt(m):
+            rows = slice(m * P, (m + 1) * P)
+            dt_sb[m] = keep.tile([P, PAIRS], BF16, name="dt%d" % m)
+            nc.sync.dma_start(out=dt_sb[m][:], in_=dt[rows, :])
+
+        def load_unit(h, d, g):
+            cols = slice(h * N, (h + 1) * N)
+            src = coarse[:, d, cols] if g == 0 else step[(g - 1) * K_PASS : g * K_PASS, d, cols]
+            raw[h, d, g] = work.tile([P, PACK, N], BF16, name="raw", tag="big", bufs=12)
+            nc.sync.dma_start(out=raw[h, d, g][:], in_=src.rearrange("(p t) n -> p t n", t=PACK))
+
+        units = [(d, g) for d in range(COMPS) for g in range(PASSES)]
+        load_weights(0)
+        for d, g in units:
+            load_unit(0, d, g)
+        load_grad(0)
+        load_weights(1)
+        load_dt(0)
+        for m in range(1, M_TILES):
+            load_grad(m)
+            if m + 1 < M_TILES:
+                load_weights(m + 1)
+            load_dt(m)
+            if m - 1 < len(units):
+                load_unit(1, *units[m - 1])
+
+        inter, x_codes, x_scales = {}, {}, {}
+
+        def interleave(key, c0, c1, on_vector):
+            if key not in inter:
+                inter[key] = work.tile([P, N * PACK], BF16, name="inter", bufs=3, align_bytes=64)
+            dst = inter[key][:, c0 * PACK : c1 * PACK].rearrange("p (c i t) -> p c t i", i=4, t=PACK)
+            src = raw[key][:, :, c0:c1].rearrange("p t (c i) -> p c t i", i=4)
+            if on_vector:
+                nc.vector.tensor_copy(out=dst, in_=src)
+            else:
+                nc.scalar.copy(out=dst, in_=src)
+
+        def quantize_unit(key):
+            name = "%d_%d_%d" % key
+            x_codes[key] = keep.tile([P, N], U32, name="xc" + name, align_bytes=64)
+            x_scales[key] = keep.tile([P, N], U8, name="xs" + name, align_bytes=64)
+            fmt = E4M3 if key[2] == 0 else E5M2
+            nc.vector.quantize_mx(out=x_codes[key][:].bitcast(fmt), scales=x_scales[key][:], in_=inter[key][:])
+
+        w_t, w_grouped, w_codes, w_scales = {}, {}, {}, {}
+
+        def transpose_weights(m):
+            wp, wa = w_raw[m]
+            bank_p = psum.tile([P, 1, 2, P], F32, name="bank_p", tag="tp")
+            bank_a = psum.tile([P, 2, 2, P], F32, name="bank_a", tag="ta")
+            words_p = wp[:].bitcast(F32)
+            words_a = wa[:].bitcast(F32)
+            for u in range(2):
+                nc.tensor.transpose(bank_p[:, 0, u, :], words_p[:, u : 256 : 2], ident[:])
+            for g in range(2):
+                for u in range(2):
+                    nc.tensor.transpose(bank_a[:, g, u, :], words_a[:, 256 * g + u : 256 * (g + 1) : 2], ident[:])
+            w_t[m] = (bank_p, bank_a)
+
+        def copy_weights(m):
+            bank_p, bank_a = w_t[m]
+            gp = work.tile([P, P * PACK], BF16, name="gp", align_bytes=64)
+            ga = work.tile([P, 2 * P * PACK], BF16, name="ga", align_bytes=64)
+            nc.scalar.copy(out=gp[:].bitcast(F32).rearrange("p (g r u) -> p g r u", g=1, u=2),
+                           in_=bank_p[:].rearrange("p g u r -> p g r u"))
+            nc.scalar.copy(out=ga[:].bitcast(F32).rearrange("p (g r u) -> p g r u", g=2, u=2),
+                           in_=bank_a[:].rearrange("p g u r -> p g r u"))
+            w_grouped[m] = (gp, ga)
+
+        def quantize_weights(m):
+            gp, ga = w_grouped[m]
+            w_codes[m] = keep.tile([P, PASSES * P], U32, name="wc%d" % m, align_bytes=64)
+            w_scales[m] = keep.tile([P, PASSES * P], U8, name="ws%d" % m, align_bytes=64)
+            nc.vector.quantize_mx(out=w_codes[m][:, :P].bitcast(E4M3), scales=w_scales[m][:, :P], in_=gp[:])
+            nc.vector.quantize_mx(out=w_codes[m][:, P:].bitcast(E4M3), scales=w_scales[m][:, P:], in_=ga[:])
+
+        fbar, t_sb, s_sb, r_sb, u_sb = {}, {}, {}, {}, {}
+
+        def matmuls(k, d):
+            h, m = divmod(k, M_TILES)
+            fbar[k, d] = psum.tile([P, N], F32, name="fbar", bufs=6)
+            for g in range(PASSES):
+                fmt = E4M3 if g == 0 else E5M2
+                cols = slice(g * P, (g + 1) * P)
+                nc.tensor.matmul_mx(
+                    out=fbar[k, d][:],
+                    lhsT=w_codes[m][:, cols].bitcast(E4M3), lhsT_scale=w_scales[m][:, cols],
+                    rhs=x_codes[h, d, g][:].bitcast(fmt), rhs_scale=x_scales[h, d, g][:],
+                    start=(g == 0), stop=(g == PASSES - 1))
+
+        def products(k, d):
+            h, m = divmod(k, M_TILES)
+            t_sb[k, d] = work.tile([P, N], F32, name="t%d" % d)
+            nc.vector.tensor_tensor(out=t_sb[k, d][:], in0=fbar[k, d][:], in1=g_sb[m][:, d, h * N : (h + 1) * N], op=MUL)
+
+        def add_dt(k):
+            h, m = divmod(k, M_TILES)
+            s_sb[k] = work.tile([P, N], F32, name="s")
+            nc.vector.tensor_tensor(out=s_sb[k][:], in0=t_sb[k, 0][:], in1=dt_sb[m][:, h * N : (h + 1) * N], op=ADD)
+
+        def open_sum(k):
+            h, m = divmod(k, M_TILES)
+            s_sb[k] = psum.tile([P, N], F32, name="q", tag="tp" if k % 2 else "ta")
+            nc.tensor.matmul(s_sb[k][:], lhsT=ident_bf[:], rhs=dt_sb[m][:, h * N : (h + 1) * N], start=True, stop=False)
+
+        def close_sum(k):
+            nc.tensor.matmul(s_sb[k][:], lhsT=ident[:], rhs=t_sb[k, 0][:], start=False, stop=True)
+
+        def residual(k):
+            h, m = divmod(k, M_TILES)
+            r_sb[k] = work.tile([P, N], F32, name="r", bufs=9)
+            nc.vector.tensor_tensor(out=r_sb[k][:], in0=s_sb[k][:], in1=t_sb[k, 1][:], op=ADD)
+            nc.sync.dma_start(out=out_1[m * P : (m + 1) * P, h * N : (h + 1) * N], in_=r_sb[k][:])
+
+        def correction(k):
+            h, m = divmod(k, M_TILES)
+            u_sb[k] = work.tile([P, COMPS, N], F32, name="u")
+            nc.gpsimd.tensor_tensor(out=u_sb[k][:], in0=g_sb[m][:, :, h * N : (h + 1) * N],
+                                    in1=r_sb[k][:].unsqueeze(1).to_broadcast([P, COMPS, N]), op=MUL)
+
+        def flows(k):
+            h, m = divmod(k, M_TILES)
+            flow = work.tile([P, COMPS, N], F32, name="flow", tag="big", bufs=12)
+            for d in range(COMPS):
+                nc.vector.tensor_tensor(out=flow[:, d, :], in0=fbar[k, d][:], in1=u_sb[k][:, d, :], op=SUB)
+            nc.sync.dma_start(out=out_0[m * P : (m + 1) * P, :, h * N : (h + 1) * N], in_=flow[:])
+
+        def last_tile(k):
+            h, m = divmod(k, M_TILES)
+            cols = slice(h * N, (h + 1) * N)
+            u0 = work.tile([P, N], F32, name="t0")
+            u1 = work.tile([P, N], F32, name="t1")
+            nc.gpsimd.tensor_tensor(out=u0[:], in0=g_sb[m][:, 0, cols], in1=r_sb[k][:], op=MUL)
+            flows(k - 1)
+            nc.vector.tensor_tensor(out=u1[:], in0=g_sb[m][:, 1, cols], in1=r_sb[k][:], op=MUL)
+            for d, u in enumerate((u0, u1)):
+                flow = work.tile([P, N], F32, name="flow", tag="big", bufs=12)
+                nc.vector.tensor_tensor(out=flow[:], in0=fbar[k, d][:], in1=u[:], op=SUB)
+                nc.sync.dma_start(out=out_0[m * P : (m + 1) * P, d, cols], in_=flow[:])
+
+        transpose_weights(0)
+        copy_weights(0)
+        for i, (d, g) in enumerate(units):
+            interleave((0, d, g), 0, V_COLS, True)
+            interleave((0, d, g), V_COLS, N, False)
+            if i == 0:
+                quantize_weights(0)
+            else:
+                quantize_unit((0,) + units[i - 1])
+            if i == PASSES:
+                matmuls(0, 0)
+        quantize_unit((0,) + units[-1])
+        matmuls(0, 1)
+        transpose_weights(1)
+        copy_weights(1)
+
+        for k in range(TILES):
+            on_pe = k >= PE_FROM
+            if on_pe:
+                open_sum(k)
+                products(k, 0)
+                close_sum(k)
+                products(k, 1)
+                flows(k - 2)
+            else:
+                if k >= 2:
+                    flows(k - 2)
+                products(k, 0)
+                products(k, 1)
+            if k + 1 < M_TILES:
+                quantize_weights(k + 1)
+            if k + 2 < M_TILES:
+                transpose_weights(k + 2)
+                copy_weights(k + 2)
+            if 0 <= k - 1 < len(units):
+                interleave((1,) + units[k - 1], 0, N, False)
+            if not on_pe:
+                add_dt(k)
+            if 0 <= k - 2 < len(units):
+                quantize_unit((1,) + units[k - 2])
+            if k + 1 < TILES:
+                matmuls(k + 1, 0)
+                matmuls(k + 1, 1)
+            residual(k)
+            if k + 1 < TILES:
+                correction(k)
+        last_tile(TILES - 1)

@@ -24,8 +24,11 @@ PASSES = (COARSE + NODES) // K_PASS
 M_TILES = NODES // P
 HALVES = PAIRS // N
 TILES = M_TILES * HALVES
-V_COLS = 256
-PE_FROM = 8
+V_COLS = 288
+R_SPLIT = 384
+F_BANKS = 6
+GROUPS = [[0], [1], [2, 3], [4, 5], [6, 7]]
+LATE_GROUPS = [[0, 1, 2, 3], [4, 5, 6, 7]]
 
 
 def tile_pyramid_horn_schunck_step_s2_kernel(tc, prolong, coarse, average, step, grad, dt, out_0, out_1):
@@ -42,24 +45,30 @@ def tile_pyramid_horn_schunck_step_s2_kernel(tc, prolong, coarse, average, step,
         nc.scalar.copy(out=ident_bf[:], in_=ident[:])
 
         w_raw, g_sb, dt_sb, raw = {}, {}, {}, {}
+        prolong_v = prolong.rearrange("(p m) c -> p m c", m=M_TILES)
+        average_v = average.rearrange("(p m) c -> p m c", m=M_TILES)
+        grad_v = grad.rearrange("(p m) d j -> p (m d) j", m=M_TILES)
+        dt_v = dt.rearrange("(p m) j -> p m j", m=M_TILES)
+        flow_v = out_0.rearrange("(p m) d j -> p m d j", m=M_TILES)
+        r_v = out_1.rearrange("(p m) j -> p m j", m=M_TILES)
 
-        def load_weights(m):
-            rows = slice(m * P, (m + 1) * P)
-            wp = keep.tile([P, COARSE], BF16, name="wp%d" % m)
-            wa = keep.tile([P, NODES], BF16, name="wa%d" % m)
-            nc.sync.dma_start(out=wp[:], in_=prolong[rows, :])
-            nc.sync.dma_start(out=wa[:], in_=average[rows, :])
-            w_raw[m] = (wp, wa)
+        def load_weights(ms):
+            wp = keep.tile([P, len(ms), COARSE], BF16, name="wp%d" % ms[0])
+            wa = keep.tile([P, len(ms), NODES], BF16, name="wa%d" % ms[0])
+            nc.sync.dma_start(out=wa[:], in_=average_v[:, ms[0] : ms[-1] + 1, :])
+            nc.sync.dma_start(out=wp[:], in_=prolong_v[:, ms[0] : ms[-1] + 1, :])
+            for i, m in enumerate(ms):
+                w_raw[m] = (wp[:, i, :], wa[:, i, :])
 
-        def load_grad(m):
-            rows = slice(m * P, (m + 1) * P)
-            g_sb[m] = keep.tile([P, COMPS, PAIRS], BF16, name="g%d" % m)
-            nc.sync.dma_start(out=g_sb[m][:], in_=grad[rows])
-
-        def load_dt(m):
-            rows = slice(m * P, (m + 1) * P)
-            dt_sb[m] = keep.tile([P, PAIRS], BF16, name="dt%d" % m)
-            nc.sync.dma_start(out=dt_sb[m][:], in_=dt[rows, :])
+        def load_grad_dt(h, ms):
+            cols = slice(h * N, (h + 1) * N)
+            gt = keep.tile([P, len(ms) * COMPS, N], BF16, name="g%d_%d" % (h, ms[0]))
+            dtt = keep.tile([P, len(ms), N], BF16, name="dt%d_%d" % (h, ms[0]))
+            nc.sync.dma_start(out=gt[:], in_=grad_v[:, ms[0] * COMPS : (ms[-1] + 1) * COMPS, cols])
+            nc.sync.dma_start(out=dtt[:], in_=dt_v[:, ms[0] : ms[-1] + 1, cols])
+            for i, m in enumerate(ms):
+                g_sb[h * M_TILES + m] = gt[:, i * COMPS : (i + 1) * COMPS, :]
+                dt_sb[h * M_TILES + m] = dtt[:, i, :]
 
         def load_unit(h, d, g):
             cols = slice(h * N, (h + 1) * N)
@@ -68,19 +77,27 @@ def tile_pyramid_horn_schunck_step_s2_kernel(tc, prolong, coarse, average, step,
             nc.sync.dma_start(out=raw[h, d, g][:], in_=src.rearrange("(p t) n -> p t n", t=PACK))
 
         units = [(d, g) for d in range(COMPS) for g in range(PASSES)]
-        load_weights(0)
-        for d, g in units:
+        load_unit(0, *units[0])
+        load_weights(GROUPS[0])
+        for d, g in units[1:]:
             load_unit(0, d, g)
-        load_grad(0)
-        load_weights(1)
-        load_dt(0)
-        for m in range(1, M_TILES):
-            load_grad(m)
-            if m + 1 < M_TILES:
-                load_weights(m + 1)
-            load_dt(m)
-            if m - 1 < len(units):
-                load_unit(1, *units[m - 1])
+        load_weights(GROUPS[1])
+        load_grad_dt(0, GROUPS[0])
+        load_weights(GROUPS[2])
+        load_grad_dt(0, GROUPS[1])
+        load_unit(1, *units[0])
+        load_grad_dt(0, GROUPS[2])
+        load_weights(GROUPS[3])
+        load_unit(1, *units[1])
+        load_unit(1, *units[2])
+        load_weights(GROUPS[4])
+        load_grad_dt(0, GROUPS[3])
+        load_unit(1, *units[3])
+        load_unit(1, *units[4])
+        load_grad_dt(0, GROUPS[4])
+        load_unit(1, *units[5])
+        for ms in LATE_GROUPS:
+            load_grad_dt(1, ms)
 
         inter, x_codes, x_scales = {}, {}, {}
 
@@ -101,43 +118,32 @@ def tile_pyramid_horn_schunck_step_s2_kernel(tc, prolong, coarse, average, step,
             fmt = E4M3 if key[2] == 0 else E5M2
             nc.vector.quantize_mx(out=x_codes[key][:].bitcast(fmt), scales=x_scales[key][:], in_=inter[key][:])
 
-        w_t, w_grouped, w_codes, w_scales = {}, {}, {}, {}
+        w_grouped, w_codes, w_scales = {}, {}, {}
 
-        def transpose_weights(m):
-            wp, wa = w_raw[m]
-            bank_p = psum.tile([P, 1, 2, P], F32, name="bank_p", tag="tp")
-            bank_a = psum.tile([P, 2, 2, P], F32, name="bank_a", tag="ta")
-            words_p = wp[:].bitcast(F32)
-            words_a = wa[:].bitcast(F32)
-            for u in range(2):
-                nc.tensor.transpose(bank_p[:, 0, u, :], words_p[:, u : 256 : 2], ident[:])
-            for g in range(2):
+        def turn_weights(m, which, bank_tag):
+            passes = (1, 2)[which]
+            words = w_raw[m][which].bitcast(F32)
+            bank = psum.tile([P, passes, 2, P], F32, name="bank", tag=bank_tag)
+            for g in range(passes):
                 for u in range(2):
-                    nc.tensor.transpose(bank_a[:, g, u, :], words_a[:, 256 * g + u : 256 * (g + 1) : 2], ident[:])
-            w_t[m] = (bank_p, bank_a)
-
-        def copy_weights(m):
-            bank_p, bank_a = w_t[m]
-            gp = work.tile([P, P * PACK], BF16, name="gp", align_bytes=64)
-            ga = work.tile([P, 2 * P * PACK], BF16, name="ga", align_bytes=64)
-            nc.scalar.copy(out=gp[:].bitcast(F32).rearrange("p (g r u) -> p g r u", g=1, u=2),
-                           in_=bank_p[:].rearrange("p g u r -> p g r u"))
-            nc.scalar.copy(out=ga[:].bitcast(F32).rearrange("p (g r u) -> p g r u", g=2, u=2),
-                           in_=bank_a[:].rearrange("p g u r -> p g r u"))
-            w_grouped[m] = (gp, ga)
+                    nc.tensor.transpose(bank[:, g, u, :], words[:, 256 * g + u : 256 * (g + 1) : 2], ident[:])
+            grouped = work.tile([P, passes * P * PACK], BF16, name="grouped%d" % which, align_bytes=64)
+            nc.scalar.copy(out=grouped[:].bitcast(F32).rearrange("p (g r u) -> p g r u", g=passes, u=2),
+                           in_=bank[:].rearrange("p g u r -> p g r u"))
+            w_grouped[m, which] = grouped
 
         def quantize_weights(m):
-            gp, ga = w_grouped[m]
+            gp, ga = w_grouped[m, 0], w_grouped[m, 1]
             w_codes[m] = keep.tile([P, PASSES * P], U32, name="wc%d" % m, align_bytes=64)
             w_scales[m] = keep.tile([P, PASSES * P], U8, name="ws%d" % m, align_bytes=64)
             nc.vector.quantize_mx(out=w_codes[m][:, :P].bitcast(E4M3), scales=w_scales[m][:, :P], in_=gp[:])
             nc.vector.quantize_mx(out=w_codes[m][:, P:].bitcast(E4M3), scales=w_scales[m][:, P:], in_=ga[:])
 
-        fbar, t_sb, s_sb, r_sb, u_sb = {}, {}, {}, {}, {}
+        fbar, t_sb, s_sb, r_sb, r_pairs, u_sb = {}, {}, {}, {}, {}, {}
 
         def matmuls(k, d):
             h, m = divmod(k, M_TILES)
-            fbar[k, d] = psum.tile([P, N], F32, name="fbar", bufs=6)
+            fbar[k, d] = psum.tile([P, N], F32, name="fbar", tag="f%d" % ((COMPS * k + d) % F_BANKS))
             for g in range(PASSES):
                 fmt = E4M3 if g == 0 else E5M2
                 cols = slice(g * P, (g + 1) * P)
@@ -148,99 +154,117 @@ def tile_pyramid_horn_schunck_step_s2_kernel(tc, prolong, coarse, average, step,
                     start=(g == 0), stop=(g == PASSES - 1))
 
         def products(k, d):
-            h, m = divmod(k, M_TILES)
             t_sb[k, d] = work.tile([P, N], F32, name="t%d" % d)
-            nc.vector.tensor_tensor(out=t_sb[k, d][:], in0=fbar[k, d][:], in1=g_sb[m][:, d, h * N : (h + 1) * N], op=MUL)
+            nc.vector.tensor_tensor(out=t_sb[k, d][:], in0=fbar[k, d][:], in1=g_sb[k][:, d, :], op=MUL)
 
         def add_dt(k):
-            h, m = divmod(k, M_TILES)
-            s_sb[k] = work.tile([P, N], F32, name="s")
-            nc.vector.tensor_tensor(out=s_sb[k][:], in0=t_sb[k, 0][:], in1=dt_sb[m][:, h * N : (h + 1) * N], op=ADD)
+            s_sb[k] = work.tile([P, N], F32, name="s", bufs=1)
+            nc.vector.tensor_tensor(out=s_sb[k][:], in0=t_sb[k, 0][:], in1=dt_sb[k], op=ADD)
 
         def open_sum(k):
-            h, m = divmod(k, M_TILES)
-            s_sb[k] = psum.tile([P, N], F32, name="q", tag="tp" if k % 2 else "ta")
-            nc.tensor.matmul(s_sb[k][:], lhsT=ident_bf[:], rhs=dt_sb[m][:, h * N : (h + 1) * N], start=True, stop=False)
+            s_sb[k] = psum.tile([P, N], F32, name="q", tag="x" if k >= M_TILES and k % 2 == 0 else "y")
+            nc.tensor.matmul(s_sb[k][:], lhsT=ident_bf[:], rhs=dt_sb[k], start=True, stop=False)
 
         def close_sum(k):
             nc.tensor.matmul(s_sb[k][:], lhsT=ident[:], rhs=t_sb[k, 0][:], start=False, stop=True)
 
-        def residual(k):
-            h, m = divmod(k, M_TILES)
-            r_sb[k] = work.tile([P, N], F32, name="r", bufs=9)
-            nc.vector.tensor_tensor(out=r_sb[k][:], in0=s_sb[k][:], in1=t_sb[k, 1][:], op=ADD)
-            nc.sync.dma_start(out=out_1[m * P : (m + 1) * P, h * N : (h + 1) * N], in_=r_sb[k][:])
+        def residual(k, c0, c1):
+            if k not in r_sb:
+                if k % 2 == 0:
+                    r_pair = work.tile([P, 2, N], F32, name="r_pair", bufs=5)
+                    r_sb[k], r_sb[k + 1] = r_pair[:, 0, :], r_pair[:, 1, :]
+                    r_pairs[k] = r_pair
+            nc.vector.tensor_tensor(out=r_sb[k][:, c0:c1], in0=s_sb[k][:, c0:c1], in1=t_sb[k, 1][:, c0:c1], op=ADD)
+
+        def store_residual(k0, k1):
+            h, m = divmod(k0, M_TILES)
+            e = k0 % 2
+            nc.sync.dma_start(out=r_v[:, m : m + k1 - k0, h * N : (h + 1) * N], in_=r_pairs[k0 - e][:, e : e + k1 - k0, :])
 
         def correction(k):
-            h, m = divmod(k, M_TILES)
             u_sb[k] = work.tile([P, COMPS, N], F32, name="u")
-            nc.gpsimd.tensor_tensor(out=u_sb[k][:], in0=g_sb[m][:, :, h * N : (h + 1) * N],
-                                    in1=r_sb[k][:].unsqueeze(1).to_broadcast([P, COMPS, N]), op=MUL)
+            nc.gpsimd.tensor_tensor(out=u_sb[k][:], in0=g_sb[k],
+                                    in1=r_sb[k].unsqueeze(1).to_broadcast([P, COMPS, N]), op=MUL)
 
         def flows(k):
             h, m = divmod(k, M_TILES)
             flow = work.tile([P, COMPS, N], F32, name="flow", tag="big", bufs=12)
             for d in range(COMPS):
                 nc.vector.tensor_tensor(out=flow[:, d, :], in0=fbar[k, d][:], in1=u_sb[k][:, d, :], op=SUB)
-            nc.sync.dma_start(out=out_0[m * P : (m + 1) * P, :, h * N : (h + 1) * N], in_=flow[:])
+            nc.sync.dma_start(out=flow_v[:, m, :, h * N : (h + 1) * N], in_=flow[:])
 
         def last_tile(k):
             h, m = divmod(k, M_TILES)
-            cols = slice(h * N, (h + 1) * N)
             u0 = work.tile([P, N], F32, name="t0")
             u1 = work.tile([P, N], F32, name="t1")
-            nc.gpsimd.tensor_tensor(out=u0[:], in0=g_sb[m][:, 0, cols], in1=r_sb[k][:], op=MUL)
+            nc.gpsimd.tensor_tensor(out=u0[:], in0=g_sb[k][:, 0, :], in1=r_sb[k], op=MUL)
             flows(k - 1)
-            nc.vector.tensor_tensor(out=u1[:], in0=g_sb[m][:, 1, cols], in1=r_sb[k][:], op=MUL)
+            nc.vector.tensor_tensor(out=u1[:], in0=g_sb[k][:, 1, :], in1=r_sb[k], op=MUL)
             for d, u in enumerate((u0, u1)):
                 flow = work.tile([P, N], F32, name="flow", tag="big", bufs=12)
                 nc.vector.tensor_tensor(out=flow[:], in0=fbar[k, d][:], in1=u[:], op=SUB)
-                nc.sync.dma_start(out=out_0[m * P : (m + 1) * P, d, cols], in_=flow[:])
+                nc.sync.dma_start(out=flow_v[:, m, d, h * N : (h + 1) * N], in_=flow[:])
 
-        transpose_weights(0)
-        copy_weights(0)
         for i, (d, g) in enumerate(units):
             interleave((0, d, g), 0, V_COLS, True)
             interleave((0, d, g), V_COLS, N, False)
             if i == 0:
-                quantize_weights(0)
+                turn_weights(0, 1, "f4")
+                turn_weights(0, 0, "f5")
             else:
                 quantize_unit((0,) + units[i - 1])
+            if i == 2:
+                quantize_weights(0)
             if i == PASSES:
                 matmuls(0, 0)
         quantize_unit((0,) + units[-1])
+        turn_weights(1, 1, "x")
+        turn_weights(1, 0, "y")
         matmuls(0, 1)
-        transpose_weights(1)
-        copy_weights(1)
+        products(0, 0)
+        quantize_weights(1)
+        turn_weights(2, 1, "f4")
+        turn_weights(2, 0, "x")
+        products(0, 1)
+        add_dt(0)
+        quantize_weights(2)
+        residual(0, 0, N)
+        matmuls(1, 0)
+        matmuls(1, 1)
+        turn_weights(3, 1, "x")
+        correction(0)
 
-        for k in range(TILES):
-            on_pe = k >= PE_FROM
-            if on_pe:
-                open_sum(k)
-                products(k, 0)
-                close_sum(k)
-                products(k, 1)
-                flows(k - 2)
-            else:
-                if k >= 2:
-                    flows(k - 2)
-                products(k, 0)
-                products(k, 1)
-            if k + 1 < M_TILES:
-                quantize_weights(k + 1)
+        for k in range(1, TILES):
+            open_sum(k)
+            products(k, 0)
+            close_sum(k)
+            products(k, 1)
+            late = (1,) + units[k - 2] if 0 <= k - 2 < len(units) else None
+            if late:
+                interleave(late, N // 2, N, False)
             if k + 2 < M_TILES:
-                transpose_weights(k + 2)
-                copy_weights(k + 2)
-            if 0 <= k - 1 < len(units):
-                interleave((1,) + units[k - 1], 0, N, False)
-            if not on_pe:
-                add_dt(k)
-            if 0 <= k - 2 < len(units):
-                quantize_unit((1,) + units[k - 2])
+                turn_weights(k + 2, 0, "x")
+            if k >= 2:
+                flows(k - 2)
+            if k - 1 < len(units):
+                interleave((1,) + units[k - 1], 0, N // 2, False)
+            if k < M_TILES:
+                residual(k, 0, R_SPLIT)
+                if late:
+                    quantize_unit(late)
+                if k + 2 < M_TILES:
+                    quantize_weights(k + 2)
+                residual(k, R_SPLIT, N)
+            else:
+                residual(k, 0, N)
+            if k >= TILES - 2:
+                store_residual(k, k + 1)
+            elif k % 2:
+                store_residual(k - 1, k + 1)
             if k + 1 < TILES:
                 matmuls(k + 1, 0)
                 matmuls(k + 1, 1)
-            residual(k)
-            if k + 1 < TILES:
+                if k + 3 < M_TILES:
+                    turn_weights(k + 3, 1, "x")
                 correction(k)
         last_tile(TILES - 1)

@@ -22,13 +22,17 @@ K_PASS = P * PACK
 N = 512
 PASSES = (COARSE + NODES) // K_PASS
 M_TILES = NODES // P
-HALVES = PAIRS // N
-TILES = M_TILES * HALVES
-V_COLS = 288
-R_SPLIT = 384
-F_BANKS = 6
-GROUPS = [[0], [1], [2, 3], [4, 5], [6, 7]]
-LATE_GROUPS = [[0, 1, 2, 3], [4, 5, 6, 7]]
+TILES = M_TILES * (PAIRS // N)
+PROLONG, AVERAGE = 0, 1
+WEIGHT_PASSES = (COARSE // K_PASS, NODES // K_PASS)
+WORDS = K_PASS // 2
+
+FLOW_LAG = 2
+FBAR_BANKS = COMPS * (FLOW_LAG + 1)
+SPLIT = 384
+BIG_BUFS = 12
+R_BUFS = 5
+STAGE_BUFS = 3
 
 
 def tile_pyramid_horn_schunck_step_s2_kernel(tc, prolong, coarse, average, step, grad, dt, out_0, out_1):
@@ -44,217 +48,240 @@ def tile_pyramid_horn_schunck_step_s2_kernel(tc, prolong, coarse, average, step,
         ident_bf = keep.tile([P, P], BF16, name="ident_bf")
         nc.scalar.copy(out=ident_bf[:], in_=ident[:])
 
-        w_raw, g_sb, dt_sb, raw = {}, {}, {}, {}
         prolong_v = prolong.rearrange("(p m) c -> p m c", m=M_TILES)
         average_v = average.rearrange("(p m) c -> p m c", m=M_TILES)
         grad_v = grad.rearrange("(p m) d j -> p (m d) j", m=M_TILES)
         dt_v = dt.rearrange("(p m) j -> p m j", m=M_TILES)
         flow_v = out_0.rearrange("(p m) d j -> p m d j", m=M_TILES)
         r_v = out_1.rearrange("(p m) j -> p m j", m=M_TILES)
+        w_raw, grad_sb, dt_sb, slab_raw = {}, {}, {}, {}
 
-        def load_weights(ms):
-            wp = keep.tile([P, len(ms), COARSE], BF16, name="wp%d" % ms[0])
-            wa = keep.tile([P, len(ms), NODES], BF16, name="wa%d" % ms[0])
-            nc.sync.dma_start(out=wa[:], in_=average_v[:, ms[0] : ms[-1] + 1, :])
-            nc.sync.dma_start(out=wp[:], in_=prolong_v[:, ms[0] : ms[-1] + 1, :])
-            for i, m in enumerate(ms):
-                w_raw[m] = (wp[:, i, :], wa[:, i, :])
+        def load_weights(m0, m1):
+            prolong_rows = keep.tile([P, m1 - m0, COARSE], BF16, name="prolong%d" % m0)
+            average_rows = keep.tile([P, m1 - m0, NODES], BF16, name="average%d" % m0)
+            nc.sync.dma_start(out=average_rows[:], in_=average_v[:, m0:m1, :])
+            nc.sync.dma_start(out=prolong_rows[:], in_=prolong_v[:, m0:m1, :])
+            for m in range(m0, m1):
+                w_raw[m, PROLONG] = prolong_rows[:, m - m0, :]
+                w_raw[m, AVERAGE] = average_rows[:, m - m0, :]
 
-        def load_grad_dt(h, ms):
-            cols = slice(h * N, (h + 1) * N)
-            gt = keep.tile([P, len(ms) * COMPS, N], BF16, name="g%d_%d" % (h, ms[0]))
-            dtt = keep.tile([P, len(ms), N], BF16, name="dt%d_%d" % (h, ms[0]))
-            nc.sync.dma_start(out=gt[:], in_=grad_v[:, ms[0] * COMPS : (ms[-1] + 1) * COMPS, cols])
-            nc.sync.dma_start(out=dtt[:], in_=dt_v[:, ms[0] : ms[-1] + 1, cols])
-            for i, m in enumerate(ms):
-                g_sb[h * M_TILES + m] = gt[:, i * COMPS : (i + 1) * COMPS, :]
-                dt_sb[h * M_TILES + m] = dtt[:, i, :]
+        def load_grad_dt(half, m0, m1):
+            cols = slice(half * N, (half + 1) * N)
+            grad_rows = keep.tile([P, (m1 - m0) * COMPS, N], BF16, name="grad%d_%d" % (half, m0))
+            dt_rows = keep.tile([P, m1 - m0, N], BF16, name="dt%d_%d" % (half, m0))
+            nc.sync.dma_start(out=grad_rows[:], in_=grad_v[:, m0 * COMPS : m1 * COMPS, cols])
+            nc.sync.dma_start(out=dt_rows[:], in_=dt_v[:, m0:m1, cols])
+            for m in range(m0, m1):
+                grad_sb[half * M_TILES + m] = grad_rows[:, (m - m0) * COMPS : (m - m0 + 1) * COMPS, :]
+                dt_sb[half * M_TILES + m] = dt_rows[:, m - m0, :]
 
-        def load_unit(h, d, g):
-            cols = slice(h * N, (h + 1) * N)
-            src = coarse[:, d, cols] if g == 0 else step[(g - 1) * K_PASS : g * K_PASS, d, cols]
-            raw[h, d, g] = work.tile([P, PACK, N], BF16, name="raw", tag="big", bufs=12)
-            nc.sync.dma_start(out=raw[h, d, g][:], in_=src.rearrange("(p t) n -> p t n", t=PACK))
+        def load_slab(slab):
+            half, d, g = slab
+            cols = slice(half * N, (half + 1) * N)
+            rows = coarse[:, d, cols] if g == 0 else step[(g - 1) * K_PASS : g * K_PASS, d, cols]
+            slab_raw[slab] = work.tile([P, PACK, N], BF16, name="slab_raw", tag="big", bufs=BIG_BUFS)
+            nc.sync.dma_start(out=slab_raw[slab][:], in_=rows.rearrange("(p t) n -> p t n", t=PACK))
 
-        units = [(d, g) for d in range(COMPS) for g in range(PASSES)]
-        load_unit(0, *units[0])
-        load_weights(GROUPS[0])
-        for d, g in units[1:]:
-            load_unit(0, d, g)
-        load_weights(GROUPS[1])
-        load_grad_dt(0, GROUPS[0])
-        load_weights(GROUPS[2])
-        load_grad_dt(0, GROUPS[1])
-        load_unit(1, *units[0])
-        load_grad_dt(0, GROUPS[2])
-        load_weights(GROUPS[3])
-        load_unit(1, *units[1])
-        load_unit(1, *units[2])
-        load_weights(GROUPS[4])
-        load_grad_dt(0, GROUPS[3])
-        load_unit(1, *units[3])
-        load_unit(1, *units[4])
-        load_grad_dt(0, GROUPS[4])
-        load_unit(1, *units[5])
-        for ms in LATE_GROUPS:
-            load_grad_dt(1, ms)
+        first_slabs = [(0, d, g) for d in range(COMPS) for g in range(PASSES)]
+        second_slabs = [(1, d, g) for d in range(COMPS) for g in range(PASSES)]
+        load_weights(0, 1)
+        for slab in first_slabs:
+            load_slab(slab)
+        load_weights(1, 2)
+        load_weights(2, 3)
+        node_groups = [(0, 1), (1, 2), (2, 4), (4, 6), (6, 8)]
+        weight_groups = [(3, 4), (4, 6), (6, 8)]
+        for i, (m0, m1) in enumerate(node_groups):
+            load_grad_dt(0, m0, m1)
+            if i < len(weight_groups):
+                load_weights(*weight_groups[i])
+            for slab in second_slabs[max(m0 - 1, 0) : m1 - 1]:
+                load_slab(slab)
+        load_grad_dt(1, 0, M_TILES // 2)
+        load_grad_dt(1, M_TILES // 2, M_TILES)
 
-        inter, x_codes, x_scales = {}, {}, {}
+        slab_words, slab_codes, slab_scales = {}, {}, {}
 
-        def interleave(key, c0, c1, on_vector):
-            if key not in inter:
-                inter[key] = work.tile([P, N * PACK], BF16, name="inter", bufs=3, align_bytes=64)
-            dst = inter[key][:, c0 * PACK : c1 * PACK].rearrange("p (c i t) -> p c t i", i=4, t=PACK)
-            src = raw[key][:, :, c0:c1].rearrange("p t (c i) -> p c t i", i=4)
-            if on_vector:
-                nc.vector.tensor_copy(out=dst, in_=src)
-            else:
-                nc.scalar.copy(out=dst, in_=src)
+        def interleave(slab, side, copy):
+            c0, c1 = side * N // 2, (side + 1) * N // 2
+            if side == 0:
+                slab_words[slab] = work.tile([P, N * PACK], BF16, name="slab_words", bufs=STAGE_BUFS, align_bytes=64)
+            copy(out=slab_words[slab][:, c0 * PACK : c1 * PACK].rearrange("p (c i t) -> p c t i", i=4, t=PACK),
+                 in_=slab_raw[slab][:, :, c0:c1].rearrange("p t (c i) -> p c t i", i=4))
 
-        def quantize_unit(key):
-            name = "%d_%d_%d" % key
-            x_codes[key] = keep.tile([P, N], U32, name="xc" + name, align_bytes=64)
-            x_scales[key] = keep.tile([P, N], U8, name="xs" + name, align_bytes=64)
-            fmt = E4M3 if key[2] == 0 else E5M2
-            nc.vector.quantize_mx(out=x_codes[key][:].bitcast(fmt), scales=x_scales[key][:], in_=inter[key][:])
+        def quantize_slab(slab):
+            name = "%d_%d_%d" % slab
+            slab_codes[slab] = keep.tile([P, N], U32, name="slab_codes" + name, align_bytes=64)
+            slab_scales[slab] = keep.tile([P, N], U8, name="slab_scales" + name, align_bytes=64)
+            nc.vector.quantize_mx(out=slab_codes[slab][:].bitcast(slab_format(slab)), scales=slab_scales[slab][:],
+                                  in_=slab_words[slab][:])
 
-        w_grouped, w_codes, w_scales = {}, {}, {}
+        def slab_format(slab):
+            return E4M3 if slab[2] == 0 else E5M2
 
-        def turn_weights(m, which, bank_tag):
-            passes = (1, 2)[which]
-            words = w_raw[m][which].bitcast(F32)
-            bank = psum.tile([P, passes, 2, P], F32, name="bank", tag=bank_tag)
+        w_words, w_codes, w_scales = {}, {}, {}
+
+        def transpose_weights(m, matrix, bank_tag):
+            passes = WEIGHT_PASSES[matrix]
+            words = w_raw[m, matrix].bitcast(F32)
+            turned = psum.tile([P, passes, 2, P], F32, name="turned", tag=bank_tag)
             for g in range(passes):
                 for u in range(2):
-                    nc.tensor.transpose(bank[:, g, u, :], words[:, 256 * g + u : 256 * (g + 1) : 2], ident[:])
-            grouped = work.tile([P, passes * P * PACK], BF16, name="grouped%d" % which, align_bytes=64)
-            nc.scalar.copy(out=grouped[:].bitcast(F32).rearrange("p (g r u) -> p g r u", g=passes, u=2),
-                           in_=bank[:].rearrange("p g u r -> p g r u"))
-            w_grouped[m, which] = grouped
+                    nc.tensor.transpose(turned[:, g, u, :], words[:, WORDS * g + u : WORDS * (g + 1) : 2], ident[:])
+            w_words[m, matrix] = work.tile([P, passes * P * PACK], BF16, name="w_words%d" % matrix,
+                                           bufs=STAGE_BUFS, align_bytes=64)
+            nc.scalar.copy(out=w_words[m, matrix][:].bitcast(F32).rearrange("p (g r u) -> p g r u", g=passes, u=2),
+                           in_=turned[:].rearrange("p g u r -> p g r u"))
 
         def quantize_weights(m):
-            gp, ga = w_grouped[m, 0], w_grouped[m, 1]
-            w_codes[m] = keep.tile([P, PASSES * P], U32, name="wc%d" % m, align_bytes=64)
-            w_scales[m] = keep.tile([P, PASSES * P], U8, name="ws%d" % m, align_bytes=64)
-            nc.vector.quantize_mx(out=w_codes[m][:, :P].bitcast(E4M3), scales=w_scales[m][:, :P], in_=gp[:])
-            nc.vector.quantize_mx(out=w_codes[m][:, P:].bitcast(E4M3), scales=w_scales[m][:, P:], in_=ga[:])
+            w_codes[m] = keep.tile([P, PASSES * P], U32, name="w_codes%d" % m, align_bytes=64)
+            w_scales[m] = keep.tile([P, PASSES * P], U8, name="w_scales%d" % m, align_bytes=64)
+            for matrix, cols in ((PROLONG, slice(0, P)), (AVERAGE, slice(P, PASSES * P))):
+                nc.vector.quantize_mx(out=w_codes[m][:, cols].bitcast(E4M3), scales=w_scales[m][:, cols],
+                                      in_=w_words[m, matrix][:])
 
-        fbar, t_sb, s_sb, r_sb, r_pairs, u_sb = {}, {}, {}, {}, {}, {}
+        fbar_tags = ["fbar%d" % i for i in range(FBAR_BANKS)]
+        free_banks = list(fbar_tags)
+        waiting = [(k, d) for k in range(TILES) for d in range(COMPS)]
+        fbar, bank_of = {}, {}
 
-        def matmuls(k, d):
-            h, m = divmod(k, M_TILES)
-            fbar[k, d] = psum.tile([P, N], F32, name="fbar", tag="f%d" % ((COMPS * k + d) % F_BANKS))
+        def mx_group(k, d):
+            half, m = divmod(k, M_TILES)
+            waiting.remove((k, d))
+            bank_of[k, d] = free_banks.pop(0)
+            fbar[k, d] = psum.tile([P, N], F32, name="fbar", tag=bank_of[k, d])
             for g in range(PASSES):
-                fmt = E4M3 if g == 0 else E5M2
+                slab = (half, d, g)
                 cols = slice(g * P, (g + 1) * P)
                 nc.tensor.matmul_mx(
                     out=fbar[k, d][:],
                     lhsT=w_codes[m][:, cols].bitcast(E4M3), lhsT_scale=w_scales[m][:, cols],
-                    rhs=x_codes[h, d, g][:].bitcast(fmt), rhs_scale=x_scales[h, d, g][:],
+                    rhs=slab_codes[slab][:].bitcast(slab_format(slab)), rhs_scale=slab_scales[slab][:],
                     start=(g == 0), stop=(g == PASSES - 1))
 
-        def products(k, d):
-            t_sb[k, d] = work.tile([P, N], F32, name="t%d" % d)
-            nc.vector.tensor_tensor(out=t_sb[k, d][:], in0=fbar[k, d][:], in1=g_sb[k][:, d, :], op=MUL)
+        def next_mx_groups():
+            for k, d in waiting[: len(free_banks)]:
+                half, m = divmod(k, M_TILES)
+                if m not in w_codes or (half, d, PASSES - 1) not in slab_codes:
+                    break
+                mx_group(k, d)
 
-        def add_dt(k):
-            s_sb[k] = work.tile([P, N], F32, name="s", bufs=1)
-            nc.vector.tensor_tensor(out=s_sb[k][:], in0=t_sb[k, 0][:], in1=dt_sb[k], op=ADD)
+        t_sb, sum_ps, sum_sb, r_pair, u_sb, flow_sb = {}, {}, {}, {}, {}, {}
+
+        def tensor_cols(k):
+            return 0 if k == 0 else SPLIT if k + 2 < M_TILES else N
+
+        def product(k, d):
+            t_sb[k, d] = work.tile([P, N], F32, name="t%d" % d)
+            nc.vector.tensor_tensor(out=t_sb[k, d][:], in0=fbar[k, d][:], in1=grad_sb[k][:, d, :], op=MUL)
 
         def open_sum(k):
-            s_sb[k] = psum.tile([P, N], F32, name="q", tag="x" if k >= M_TILES and k % 2 == 0 else "y")
-            nc.tensor.matmul(s_sb[k][:], lhsT=ident_bf[:], rhs=dt_sb[k], start=True, stop=False)
+            cols = slice(0, tensor_cols(k))
+            sum_ps[k] = psum.tile([P, N], F32, name="sum_ps", tag="sum")
+            nc.tensor.matmul(sum_ps[k][:, cols], lhsT=ident_bf[:], rhs=dt_sb[k][:, cols], start=True, stop=False)
 
         def close_sum(k):
-            nc.tensor.matmul(s_sb[k][:], lhsT=ident[:], rhs=t_sb[k, 0][:], start=False, stop=True)
+            cols = slice(0, tensor_cols(k))
+            nc.tensor.matmul(sum_ps[k][:, cols], lhsT=ident[:], rhs=t_sb[k, 0][:, cols], start=False, stop=True)
+
+        def vector_sum(k):
+            cols = slice(tensor_cols(k), N)
+            sum_sb[k] = work.tile([P, N], F32, name="sum_sb", bufs=1)
+            nc.vector.tensor_tensor(out=sum_sb[k][:, cols], in0=t_sb[k, 0][:, cols], in1=dt_sb[k][:, cols], op=ADD)
+
+        def r_rows(k):
+            return r_pair[k // 2][:, k % 2, :]
 
         def residual(k, c0, c1):
-            if k not in r_sb:
-                if k % 2 == 0:
-                    r_pair = work.tile([P, 2, N], F32, name="r_pair", bufs=5)
-                    r_sb[k], r_sb[k + 1] = r_pair[:, 0, :], r_pair[:, 1, :]
-                    r_pairs[k] = r_pair
-            nc.vector.tensor_tensor(out=r_sb[k][:, c0:c1], in0=s_sb[k][:, c0:c1], in1=t_sb[k, 1][:, c0:c1], op=ADD)
+            if k // 2 not in r_pair:
+                r_pair[k // 2] = work.tile([P, 2, N], F32, name="r_pair", bufs=R_BUFS)
+            partial = sum_ps[k] if c0 < tensor_cols(k) else sum_sb[k]
+            nc.vector.tensor_tensor(out=r_rows(k)[:, c0:c1], in0=partial[:, c0:c1], in1=t_sb[k, 1][:, c0:c1], op=ADD)
 
         def store_residual(k0, k1):
-            h, m = divmod(k0, M_TILES)
-            e = k0 % 2
-            nc.sync.dma_start(out=r_v[:, m : m + k1 - k0, h * N : (h + 1) * N], in_=r_pairs[k0 - e][:, e : e + k1 - k0, :])
+            half, m = divmod(k0, M_TILES)
+            nc.sync.dma_start(out=r_v[:, m : m + k1 - k0, half * N : (half + 1) * N],
+                              in_=r_pair[k0 // 2][:, k0 % 2 : k0 % 2 + k1 - k0, :])
 
         def correction(k):
             u_sb[k] = work.tile([P, COMPS, N], F32, name="u")
-            nc.gpsimd.tensor_tensor(out=u_sb[k][:], in0=g_sb[k],
-                                    in1=r_sb[k].unsqueeze(1).to_broadcast([P, COMPS, N]), op=MUL)
+            nc.gpsimd.tensor_tensor(out=u_sb[k][:], in0=grad_sb[k],
+                                    in1=r_rows(k).unsqueeze(1).to_broadcast([P, COMPS, N]), op=MUL)
 
-        def flows(k):
-            h, m = divmod(k, M_TILES)
-            flow = work.tile([P, COMPS, N], F32, name="flow", tag="big", bufs=12)
-            for d in range(COMPS):
-                nc.vector.tensor_tensor(out=flow[:, d, :], in0=fbar[k, d][:], in1=u_sb[k][:, d, :], op=SUB)
-            nc.sync.dma_start(out=flow_v[:, m, :, h * N : (h + 1) * N], in_=flow[:])
+        def flow(k, d):
+            half, m = divmod(k, M_TILES)
+            if d == 0:
+                flow_sb[k] = work.tile([P, COMPS, N], F32, name="flow", tag="big", bufs=BIG_BUFS)
+            nc.vector.tensor_tensor(out=flow_sb[k][:, d, :], in0=fbar[k, d][:], in1=u_sb[k][:, d, :], op=SUB)
+            free_banks.append(bank_of[k, d])
+            if d == COMPS - 1:
+                nc.sync.dma_start(out=flow_v[:, m, :, half * N : (half + 1) * N], in_=flow_sb[k][:])
 
-        def last_tile(k):
-            h, m = divmod(k, M_TILES)
-            u0 = work.tile([P, N], F32, name="t0")
-            u1 = work.tile([P, N], F32, name="t1")
-            nc.gpsimd.tensor_tensor(out=u0[:], in0=g_sb[k][:, 0, :], in1=r_sb[k], op=MUL)
-            flows(k - 1)
-            nc.vector.tensor_tensor(out=u1[:], in0=g_sb[k][:, 1, :], in1=r_sb[k], op=MUL)
-            for d, u in enumerate((u0, u1)):
-                flow = work.tile([P, N], F32, name="flow", tag="big", bufs=12)
-                nc.vector.tensor_tensor(out=flow[:], in0=fbar[k, d][:], in1=u[:], op=SUB)
-                nc.sync.dma_start(out=flow_v[:, m, d, h * N : (h + 1) * N], in_=flow[:])
-
-        for i, (d, g) in enumerate(units):
-            interleave((0, d, g), 0, V_COLS, True)
-            interleave((0, d, g), V_COLS, N, False)
+        spare_banks = fbar_tags[-2:]
+        transpose_weights(0, AVERAGE, spare_banks[0])
+        transpose_weights(0, PROLONG, spare_banks[1])
+        for i, slab in enumerate(first_slabs):
+            interleave(slab, 0, nc.vector.tensor_copy)
+            interleave(slab, 1, nc.scalar.copy)
             if i == 0:
-                turn_weights(0, 1, "f4")
-                turn_weights(0, 0, "f5")
-            else:
-                quantize_unit((0,) + units[i - 1])
-            if i == 2:
                 quantize_weights(0)
-            if i == PASSES:
-                matmuls(0, 0)
-        quantize_unit((0,) + units[-1])
-        turn_weights(1, 1, "x")
-        turn_weights(1, 0, "y")
-        matmuls(0, 1)
-        products(0, 0)
+            else:
+                quantize_slab(first_slabs[i - 1])
+            next_mx_groups()
+        quantize_slab(first_slabs[-1])
+        transpose_weights(1, AVERAGE, "turn")
+        transpose_weights(1, PROLONG, "sum")
+        transpose_weights(2, AVERAGE, spare_banks[0])
+        transpose_weights(2, PROLONG, spare_banks[1])
+        next_mx_groups()
+        product(0, 0)
         quantize_weights(1)
-        turn_weights(2, 1, "f4")
-        turn_weights(2, 0, "x")
-        products(0, 1)
-        add_dt(0)
+        product(0, 1)
+        vector_sum(0)
         quantize_weights(2)
         residual(0, 0, N)
-        matmuls(1, 0)
-        matmuls(1, 1)
-        turn_weights(3, 1, "x")
+        mx_group(1, 0)
+        mx_group(1, 1)
+        transpose_weights(3, AVERAGE, "turn")
         correction(0)
+        open_sum(1)
+
+        sides_left = [(slab, side) for slab in second_slabs for side in range(2)]
+
+        def scalar_interleaves(count):
+            for slab, side in sides_left[:count]:
+                interleave(slab, side, nc.scalar.copy)
+                sides_left.remove((slab, side))
 
         for k in range(1, TILES):
-            open_sum(k)
-            products(k, 0)
+            prolong_tile, average_tile = k + 2, k + 3
+            product(k, 0)
             close_sum(k)
-            products(k, 1)
-            late = (1,) + units[k - 2] if 0 <= k - 2 < len(units) else None
-            if late:
-                interleave(late, N // 2, N, False)
-            if k + 2 < M_TILES:
-                turn_weights(k + 2, 0, "x")
-            if k >= 2:
-                flows(k - 2)
-            if k - 1 < len(units):
-                interleave((1,) + units[k - 1], 0, N // 2, False)
-            if k < M_TILES:
-                residual(k, 0, R_SPLIT)
-                if late:
-                    quantize_unit(late)
-                if k + 2 < M_TILES:
-                    quantize_weights(k + 2)
-                residual(k, R_SPLIT, N)
+            if k > 1:
+                scalar_interleaves(1 if prolong_tile < M_TILES else 2)
+            slabs_ready = [slab for slab in second_slabs
+                           if slab in slab_words and slab not in slab_codes and (slab, 1) not in sides_left]
+            if prolong_tile < M_TILES:
+                transpose_weights(prolong_tile, PROLONG, "turn")
+            elif prolong_tile == M_TILES:
+                free_banks.append("turn")
+            if k >= FLOW_LAG:
+                flow(k - FLOW_LAG, 0)
+            next_mx_groups()
+            product(k, 1)
+            if k >= FLOW_LAG:
+                flow(k - FLOW_LAG, 1)
+            next_mx_groups()
+            scalar_interleaves(1 if average_tile < M_TILES else 2)
+            if slabs_ready or prolong_tile < M_TILES:
+                residual(k, 0, SPLIT)
+                if tensor_cols(k) < N:
+                    vector_sum(k)
+                for slab in slabs_ready:
+                    quantize_slab(slab)
+                if prolong_tile < M_TILES:
+                    quantize_weights(prolong_tile)
+                residual(k, SPLIT, N)
             else:
                 residual(k, 0, N)
             if k >= TILES - 2:
@@ -262,9 +289,21 @@ def tile_pyramid_horn_schunck_step_s2_kernel(tc, prolong, coarse, average, step,
             elif k % 2:
                 store_residual(k - 1, k + 1)
             if k + 1 < TILES:
-                matmuls(k + 1, 0)
-                matmuls(k + 1, 1)
-                if k + 3 < M_TILES:
-                    turn_weights(k + 3, 1, "x")
+                next_mx_groups()
+                if average_tile < M_TILES:
+                    transpose_weights(average_tile, AVERAGE, "turn")
                 correction(k)
-        last_tile(TILES - 1)
+                open_sum(k + 1)
+
+        last = TILES - 1
+        half, m = divmod(last, M_TILES)
+        u_last = []
+        for d in range(COMPS):
+            flow(last - 1, d)
+            u_d = work.tile([P, N], F32, name="u_last", tag="t%d" % d)
+            nc.vector.tensor_tensor(out=u_d[:], in0=grad_sb[last][:, d, :], in1=r_rows(last), op=MUL)
+            u_last.append(u_d)
+        for d in range(COMPS):
+            flow_d = work.tile([P, N], F32, name="flow_last", tag="big", bufs=BIG_BUFS)
+            nc.vector.tensor_tensor(out=flow_d[:], in0=fbar[last, d][:], in1=u_last[d][:], op=SUB)
+            nc.sync.dma_start(out=flow_v[:, m, d, half * N : (half + 1) * N], in_=flow_d[:])

from contextlib import ExitStack

import concourse.mybir as mybir
from concourse.masks import make_identity

F32 = mybir.dt.float32
BF16 = mybir.dt.bfloat16
U32 = mybir.dt.uint32
U8 = mybir.dt.uint8
E4M3 = mybir.dt.float8_e4m3fn_x4
E5M2 = mybir.dt.float8_e5m2_x4
ADD = mybir.AluOpType.add
SUB = mybir.AluOpType.subtract
MUL = mybir.AluOpType.mult

NODES, COARSE, COMPS, PAIRS = 1024, 512, 2, 1024
FLOPS = 2 * NODES * COMPS * PAIRS * (COARSE + NODES)

P = 128
PACK = 4
K_PASS = P * PACK
N = 512
PASSES = (COARSE + NODES) // K_PASS
M_TILES = NODES // P
TILES = M_TILES * (PAIRS // N)
PROLONG, AVERAGE = 0, 1
WEIGHT_PASSES = (COARSE // K_PASS, NODES // K_PASS)
WORDS = K_PASS // 2

FLOW_LAG = 2
FBAR_BANKS = COMPS * (FLOW_LAG + 1)
SPLIT = 384
BIG_BUFS = 12
R_BUFS = 5
STAGE_BUFS = 3


def tile_pyramid_horn_schunck_step_s2_kernel(tc, prolong, coarse, average, step, grad, dt, out_0, out_1):
    nc = tc.nc
    with ExitStack() as ctx:
        keep = ctx.enter_context(tc.tile_pool(name="keep", bufs=1))
        work = ctx.enter_context(tc.tile_pool(name="work", bufs=2))
        psum = ctx.enter_context(tc.psum_pool(name="psum", bufs=1))
        ctx.enter_context(tc.manual_schedule())

        ident = keep.tile([P, P], F32, name="ident")
        make_identity(nc, ident[:])
        ident_bf = keep.tile([P, P], BF16, name="ident_bf")
        nc.scalar.copy(out=ident_bf[:], in_=ident[:])

        prolong_v = prolong.rearrange("(p m) c -> p m c", m=M_TILES)
        average_v = average.rearrange("(p m) c -> p m c", m=M_TILES)
        grad_v = grad.rearrange("(p m) d j -> p (m d) j", m=M_TILES)
        dt_v = dt.rearrange("(p m) j -> p m j", m=M_TILES)
        flow_v = out_0.rearrange("(p m) d j -> p m d j", m=M_TILES)
        r_v = out_1.rearrange("(p m) j -> p m j", m=M_TILES)
        w_raw, grad_sb, dt_sb, slab_raw = {}, {}, {}, {}

        def load_weights(m0, m1):
            prolong_rows = keep.tile([P, m1 - m0, COARSE], BF16, name="prolong%d" % m0)
            average_rows = keep.tile([P, m1 - m0, NODES], BF16, name="average%d" % m0)
            nc.sync.dma_start(out=average_rows[:], in_=average_v[:, m0:m1, :])
            nc.sync.dma_start(out=prolong_rows[:], in_=prolong_v[:, m0:m1, :])
            for m in range(m0, m1):
                w_raw[m, PROLONG] = prolong_rows[:, m - m0, :]
                w_raw[m, AVERAGE] = average_rows[:, m - m0, :]

        def load_grad_dt(half, m0, m1):
            cols = slice(half * N, (half + 1) * N)
            grad_rows = keep.tile([P, (m1 - m0) * COMPS, N], BF16, name="grad%d_%d" % (half, m0))
            dt_rows = keep.tile([P, m1 - m0, N], BF16, name="dt%d_%d" % (half, m0))
            nc.sync.dma_start(out=grad_rows[:], in_=grad_v[:, m0 * COMPS : m1 * COMPS, cols])
            nc.sync.dma_start(out=dt_rows[:], in_=dt_v[:, m0:m1, cols])
            for m in range(m0, m1):
                grad_sb[half * M_TILES + m] = grad_rows[:, (m - m0) * COMPS : (m - m0 + 1) * COMPS, :]
                dt_sb[half * M_TILES + m] = dt_rows[:, m - m0, :]

        def load_slab(slab):
            half, d, g = slab
            cols = slice(half * N, (half + 1) * N)
            rows = coarse[:, d, cols] if g == 0 else step[(g - 1) * K_PASS : g * K_PASS, d, cols]
            slab_raw[slab] = work.tile([P, PACK, N], BF16, name="slab_raw", tag="big", bufs=BIG_BUFS)
            nc.sync.dma_start(out=slab_raw[slab][:], in_=rows.rearrange("(p t) n -> p t n", t=PACK))

        first_slabs = [(0, d, g) for d in range(COMPS) for g in range(PASSES)]
        second_slabs = [(1, d, g) for d in range(COMPS) for g in range(PASSES)]
        load_weights(0, 1)
        for slab in first_slabs:
            load_slab(slab)
        load_weights(1, 2)
        load_weights(2, 3)
        node_groups = [(0, 1), (1, 2), (2, 4), (4, 6), (6, 8)]
        weight_groups = [(3, 4), (4, 6), (6, 8)]
        for i, (m0, m1) in enumerate(node_groups):
            load_grad_dt(0, m0, m1)
            if i < len(weight_groups):
                load_weights(*weight_groups[i])
            for slab in second_slabs[max(m0 - 1, 0) : m1 - 1]:
                load_slab(slab)
        load_grad_dt(1, 0, M_TILES // 2)
        load_grad_dt(1, M_TILES // 2, M_TILES)

        slab_words, slab_codes, slab_scales = {}, {}, {}

        def interleave(slab, side, copy):
            c0, c1 = side * N // 2, (side + 1) * N // 2
            if side == 0:
                slab_words[slab] = work.tile([P, N * PACK], BF16, name="slab_words", bufs=STAGE_BUFS, align_bytes=64)
            copy(out=slab_words[slab][:, c0 * PACK : c1 * PACK].rearrange("p (c i t) -> p c t i", i=4, t=PACK),
                 in_=slab_raw[slab][:, :, c0:c1].rearrange("p t (c i) -> p c t i", i=4))

        def quantize_slab(slab):
            name = "%d_%d_%d" % slab
            slab_codes[slab] = keep.tile([P, N], U32, name="slab_codes" + name, align_bytes=64)
            slab_scales[slab] = keep.tile([P, N], U8, name="slab_scales" + name, align_bytes=64)
            nc.vector.quantize_mx(out=slab_codes[slab][:].bitcast(slab_format(slab)), scales=slab_scales[slab][:],
                                  in_=slab_words[slab][:])

        def slab_format(slab):
            return E4M3 if slab[2] == 0 else E5M2

        w_words, w_codes, w_scales = {}, {}, {}

        def transpose_weights(m, matrix, bank_tag):
            passes = WEIGHT_PASSES[matrix]
            words = w_raw[m, matrix].bitcast(F32)
            turned = psum.tile([P, passes, 2, P], F32, name="turned", tag=bank_tag)
            for g in range(passes):
                for u in range(2):
                    nc.tensor.transpose(turned[:, g, u, :], words[:, WORDS * g + u : WORDS * (g + 1) : 2], ident[:])
            w_words[m, matrix] = work.tile([P, passes * P * PACK], BF16, name="w_words%d" % matrix,
                                           bufs=STAGE_BUFS, align_bytes=64)
            nc.scalar.copy(out=w_words[m, matrix][:].bitcast(F32).rearrange("p (g r u) -> p g r u", g=passes, u=2),
                           in_=turned[:].rearrange("p g u r -> p g r u"))

        def quantize_weights(m):
            w_codes[m] = keep.tile([P, PASSES * P], U32, name="w_codes%d" % m, align_bytes=64)
            w_scales[m] = keep.tile([P, PASSES * P], U8, name="w_scales%d" % m, align_bytes=64)
            for matrix, cols in ((PROLONG, slice(0, P)), (AVERAGE, slice(P, PASSES * P))):
                nc.vector.quantize_mx(out=w_codes[m][:, cols].bitcast(E4M3), scales=w_scales[m][:, cols],
                                      in_=w_words[m, matrix][:])

        fbar_tags = ["fbar%d" % i for i in range(FBAR_BANKS)]
        free_banks = list(fbar_tags)
        waiting = [(k, d) for k in range(TILES) for d in range(COMPS)]
        fbar, bank_of = {}, {}

        def mx_group(k, d):
            half, m = divmod(k, M_TILES)
            waiting.remove((k, d))
            bank_of[k, d] = free_banks.pop(0)
            fbar[k, d] = psum.tile([P, N], F32, name="fbar", tag=bank_of[k, d])
            for g in range(PASSES):
                slab = (half, d, g)
                cols = slice(g * P, (g + 1) * P)
                nc.tensor.matmul_mx(
                    out=fbar[k, d][:],
                    lhsT=w_codes[m][:, cols].bitcast(E4M3), lhsT_scale=w_scales[m][:, cols],
                    rhs=slab_codes[slab][:].bitcast(slab_format(slab)), rhs_scale=slab_scales[slab][:],
                    start=(g == 0), stop=(g == PASSES - 1))

        def next_mx_groups():
            for k, d in waiting[: len(free_banks)]:
                half, m = divmod(k, M_TILES)
                if m not in w_codes or (half, d, PASSES - 1) not in slab_codes:
                    break
                mx_group(k, d)

        t_sb, sum_ps, sum_sb, r_pair, u_sb, flow_sb = {}, {}, {}, {}, {}, {}

        def tensor_cols(k):
            return 0 if k == 0 else SPLIT if k + 2 < M_TILES else N

        def product(k, d):
            t_sb[k, d] = work.tile([P, N], F32, name="t%d" % d)
            nc.vector.tensor_tensor(out=t_sb[k, d][:], in0=fbar[k, d][:], in1=grad_sb[k][:, d, :], op=MUL)

        def open_sum(k):
            cols = slice(0, tensor_cols(k))
            sum_ps[k] = psum.tile([P, N], F32, name="sum_ps", tag="sum")
            nc.tensor.matmul(sum_ps[k][:, cols], lhsT=ident_bf[:], rhs=dt_sb[k][:, cols], start=True, stop=False)

        def close_sum(k):
            cols = slice(0, tensor_cols(k))
            nc.tensor.matmul(sum_ps[k][:, cols], lhsT=ident[:], rhs=t_sb[k, 0][:, cols], start=False, stop=True)

        def vector_sum(k):
            cols = slice(tensor_cols(k), N)
            sum_sb[k] = work.tile([P, N], F32, name="sum_sb", bufs=1)
            nc.vector.tensor_tensor(out=sum_sb[k][:, cols], in0=t_sb[k, 0][:, cols], in1=dt_sb[k][:, cols], op=ADD)

        def r_rows(k):
            return r_pair[k // 2][:, k % 2, :]

        def residual(k, c0, c1):
            if k // 2 not in r_pair:
                r_pair[k // 2] = work.tile([P, 2, N], F32, name="r_pair", bufs=R_BUFS)
            partial = sum_ps[k] if c0 < tensor_cols(k) else sum_sb[k]
            nc.vector.tensor_tensor(out=r_rows(k)[:, c0:c1], in0=partial[:, c0:c1], in1=t_sb[k, 1][:, c0:c1], op=ADD)

        def store_residual(k0, k1):
            half, m = divmod(k0, M_TILES)
            nc.sync.dma_start(out=r_v[:, m : m + k1 - k0, half * N : (half + 1) * N],
                              in_=r_pair[k0 // 2][:, k0 % 2 : k0 % 2 + k1 - k0, :])

        def correction(k):
            u_sb[k] = work.tile([P, COMPS, N], F32, name="u")
            nc.gpsimd.tensor_tensor(out=u_sb[k][:], in0=grad_sb[k],
                                    in1=r_rows(k).unsqueeze(1).to_broadcast([P, COMPS, N]), op=MUL)

        def flow(k, d):
            half, m = divmod(k, M_TILES)
            if d == 0:
                flow_sb[k] = work.tile([P, COMPS, N], F32, name="flow", tag="big", bufs=BIG_BUFS)
            nc.vector.tensor_tensor(out=flow_sb[k][:, d, :], in0=fbar[k, d][:], in1=u_sb[k][:, d, :], op=SUB)
            free_banks.append(bank_of[k, d])
            if d == COMPS - 1:
                nc.sync.dma_start(out=flow_v[:, m, :, half * N : (half + 1) * N], in_=flow_sb[k][:])

        spare_banks = fbar_tags[-2:]
        transpose_weights(0, AVERAGE, spare_banks[0])
        transpose_weights(0, PROLONG, spare_banks[1])
        for i, slab in enumerate(first_slabs):
            interleave(slab, 0, nc.vector.tensor_copy)
            interleave(slab, 1, nc.scalar.copy)
            if i == 0:
                quantize_weights(0)
            else:
                quantize_slab(first_slabs[i - 1])
            next_mx_groups()
        quantize_slab(first_slabs[-1])
        transpose_weights(1, AVERAGE, "turn")
        transpose_weights(1, PROLONG, "sum")
        transpose_weights(2, AVERAGE, spare_banks[0])
        transpose_weights(2, PROLONG, spare_banks[1])
        next_mx_groups()
        product(0, 0)
        quantize_weights(1)
        product(0, 1)
        vector_sum(0)
        quantize_weights(2)
        residual(0, 0, N)
        mx_group(1, 0)
        mx_group(1, 1)
        transpose_weights(3, AVERAGE, "turn")
        correction(0)
        open_sum(1)

        sides_left = [(slab, side) for slab in second_slabs for side in range(2)]

        def scalar_interleaves(count):
            for slab, side in sides_left[:count]:
                interleave(slab, side, nc.scalar.copy)
                sides_left.remove((slab, side))

        for k in range(1, TILES):
            prolong_tile, average_tile = k + 2, k + 3
            product(k, 0)
            close_sum(k)
            if k > 1:
                scalar_interleaves(1 if prolong_tile < M_TILES else 2)
            slabs_ready = [slab for slab in second_slabs
                           if slab in slab_words and slab not in slab_codes and (slab, 1) not in sides_left]
            if prolong_tile < M_TILES:
                transpose_weights(prolong_tile, PROLONG, "turn")
            elif prolong_tile == M_TILES:
                free_banks.append("turn")
            if k >= FLOW_LAG:
                flow(k - FLOW_LAG, 0)
            next_mx_groups()
            product(k, 1)
            if k >= FLOW_LAG:
                flow(k - FLOW_LAG, 1)
            next_mx_groups()
            scalar_interleaves(1 if average_tile < M_TILES else 2)
            if slabs_ready or prolong_tile < M_TILES:
                residual(k, 0, SPLIT)
                if tensor_cols(k) < N:
                    vector_sum(k)
                for slab in slabs_ready:
                    quantize_slab(slab)
                if prolong_tile < M_TILES:
                    quantize_weights(prolong_tile)
                residual(k, SPLIT, N)
            else:
                residual(k, 0, N)
            if k >= TILES - 2:
                store_residual(k, k + 1)
            elif k % 2:
                store_residual(k - 1, k + 1)
            if k + 1 < TILES:
                next_mx_groups()
                if average_tile < M_TILES:
                    transpose_weights(average_tile, AVERAGE, "turn")
                correction(k)
                open_sum(k + 1)

        last = TILES - 1
        half, m = divmod(last, M_TILES)
        u_last = []
        for d in range(COMPS):
            flow(last - 1, d)
            u_d = work.tile([P, N], F32, name="u_last", tag="t%d" % d)
            nc.vector.tensor_tensor(out=u_d[:], in0=grad_sb[last][:, d, :], in1=r_rows(last), op=MUL)
            u_last.append(u_d)
        for d in range(COMPS):
            flow_d = work.tile([P, N], F32, name="flow_last", tag="big", bufs=BIG_BUFS)
            nc.vector.tensor_tensor(out=flow_d[:], in0=fbar[last, d][:], in1=u_last[d][:], op=SUB)
            nc.sync.dma_start(out=flow_v[:, m, d, half * N : (half + 1) * N], in_=flow_d[:])
